import numpy as np
import ml_dtypes


def mxq(x, axis, fmt="e4m3"):
    dtype, down = {"e4m3": (ml_dtypes.float8_e4m3fn, 7), "e5m2": (ml_dtypes.float8_e5m2, 14)}[fmt]
    v = np.moveaxis(np.asarray(x, np.float32).astype(ml_dtypes.bfloat16).astype(np.float64), axis, -1)
    blocks = v.reshape(v.shape[:-1] + (-1, 32))
    amax = np.abs(blocks).max(-1, keepdims=True)
    byte = np.maximum(np.where(amax > 0, np.frexp(amax)[1] - 1 + 127, 0) - down, 1)
    scale = np.exp2(byte - 127.0)
    codes = (blocks / scale).astype(np.float32).astype(dtype).astype(np.float64)
    return np.moveaxis((codes * scale).reshape(v.shape), -1, axis)


WIDE = False


def mx_kscale(k):
    if not WIDE:
        return np.ones(k)
    levels = np.array([30, -30])
    if k % 512:
        return np.exp2(np.random.permutation(np.resize(levels, k // 32))).repeat(32)
    a = np.empty((k // 512, 16))
    for p in range(k // 512):
        a[p, :8] = np.random.permutation(np.resize(levels, 8))
        for g in range(8):
            far = levels[np.abs(levels - a[p, g]) >= 10]
            a[p, g + 8] = far[np.random.randint(len(far))]
    return np.exp2(a.ravel()).repeat(32)


BF16 = ml_dtypes.bfloat16


def bf(x):
    return np.asarray(x, np.float32).astype(BF16)


def f64(x):
    return np.asarray(x).astype(np.float64)


E2M1 = np.array([0.0, 0.5, 1.0, 1.5, 2.0, 3.0, 4.0, 6.0, -0.0, -0.5, -1.0, -1.5, -2.0, -3.0, -4.0, -6.0])


def pack_weight(w, fmt):
    k, n = w.shape
    w = f64(bf(w)).reshape(k // 32, 32, n)
    amax = np.abs(w).max(1)
    if fmt == "e4m3":
        byte = np.frexp(amax)[1] - 1 + 127 - 7
    else:
        mant, ex = np.frexp(amax / 6.0)
        byte = np.where(mant > 0.5, ex, ex - 1) + 127
    byte = np.clip(np.where(amax > 0, byte, 1), 1, 254)
    scaled = (w * np.exp2(127.0 - byte)[:, None, :]).reshape(k, n).astype(np.float32)
    by_word = np.ascontiguousarray(scaled.reshape(k // 512, 128, 4, n).transpose(0, 1, 3, 2))
    if fmt == "e4m3":
        words = by_word.astype(ml_dtypes.float8_e4m3fn).view(np.uint8)
    else:
        c = by_word.astype(ml_dtypes.float4_e2m1fn).view(np.uint8) & 0xF
        words = c[..., 0::2] | (c[..., 1::2] << 4)
    return np.ascontiguousarray(words), np.ascontiguousarray(byte.astype(np.uint8).reshape(k // 512, 16, n))


def unpack_weight(words, scales, fmt):
    g, p, n, _ = words.shape
    if fmt == "e4m3":
        vals = np.ascontiguousarray(words).view(ml_dtypes.float8_e4m3fn).astype(np.float64)
    else:
        nib = np.empty((g, p, n, 4), np.uint8)
        nib[..., 0::2] = words & 0xF
        nib[..., 1::2] = words >> 4
        vals = E2M1[nib]
    vals = vals * np.repeat(np.exp2(scales.astype(np.float64) - 127.0), 8, axis=1)[..., None]
    return vals.transpose(0, 1, 3, 2).reshape(g * 512, n)
def pack4(w):
    words, scales = pack_weight(w, "e2m1")
    return words.reshape(words.shape[0], 128, -1), scales


def unpack4(words, scales):
    return unpack_weight(words.reshape(words.shape[0], 128, -1, 2), scales, "e2m1")


T, E, C, D = 2048, 1024, 512, 1536


def setup_inputs():
    s = mx_kscale(E)
    t = mx_kscale(T)
    w = np.random.standard_normal((E, C)) / np.sqrt(E) / s[:, None]
    w_words, w_scales = pack4(w)
    common = np.random.standard_normal(E)
    return {
        "x": bf((np.random.standard_normal((T, E)) + common) * s),
        "w_words": w_words,
        "w_scales": w_scales,
        "m": bf(np.exp(0.25 * np.random.standard_normal(T)) * t),
        "v": bf(np.random.standard_normal((T, D)) / np.sqrt(D) / t[:, None]),
        "c": bf(2.0 * np.random.standard_normal((C, D)) / T),
    }


def reference(x, w_words, w_scales, m, v, c):
    z = mxq(f64(x), 1, "e4m3") @ unpack4(w_words, w_scales)
    a = 1.0 / (1.0 + np.exp(-z))
    r = a * f64(m)[:, None]
    sums = mxq(r, 0, "e5m2").T @ mxq(f64(v), 0, "e4m3")
    mass = a.sum(axis=0)
    return sums - mass[:, None] * f64(c)

@@ -1,0 +1,265 @@
+from contextlib import ExitStack
+
+import concourse.mybir as mybir
+from concourse.masks import make_identity
+
+T, E, C, D = 2048, 1024, 512, 1536
+FLOPS = 2 * T * E * C + 2 * T * C * D
+
+F32 = mybir.dt.float32
+BF16 = mybir.dt.bfloat16
+I32 = mybir.dt.int32
+U32 = mybir.dt.uint32
+U8 = mybir.dt.uint8
+E4M3 = mybir.dt.float8_e4m3fn_x4
+E5M2 = mybir.dt.float8_e5m2_x4
+E2M1 = mybir.dt.float4_e2m1fn_x4
+ACT = mybir.ActivationFunctionType
+ALU = mybir.AluOpType
+
+P = 128
+PACK = 4
+K_PASS = P * PACK
+N = 512
+GROUPS = T // K_PASS
+E_PASSES = E // K_PASS
+C_TILES = C // P
+D_TILES = D // N
+STEPS = GROUPS * C_TILES
+X_AHEAD = 6
+V_PIECES = 4
+V_COLS = N // V_PIECES
+X_BANKS = (0, 1, 6)
+Z_BANKS = (2, 3)
+A_BANKS = (4, 5)
+S_BANKS = ((0, 1, 6, 7), (2, 3, 4, 5), (0, 1, 6, 7))
+
+
+def tile_netvlad_length_pooling_s9_kernel(tc, x, w_words, w_scales, m, v, c, out):
+    nc = tc.nc
+    with ExitStack() as ctx:
+        keep = ctx.enter_context(tc.tile_pool(name="keep", bufs=1))
+        stage = ctx.enter_context(tc.tile_pool(name="stage", bufs=3))
+        psum = ctx.enter_context(tc.psum_pool(name="psum", bufs=1))
+        ctx.enter_context(tc.manual_schedule())
+
+        def bank(b):
+            return psum.tile([P, N], F32, name="bank%d" % b)
+
+        ident = keep.tile([P, P], F32, name="ident")
+        make_identity(nc, ident[:])
+
+        w_codes = keep.tile([P, E_PASSES, 2 * C], U8, name="w_codes", align_bytes=64)
+        w_plane = keep.tile([P, E_PASSES, C], U8, name="w_plane", align_bytes=64)
+        lengths = keep.tile([P, GROUPS, PACK], BF16, name="lengths")
+        mass_parts = keep.tile([P, C_TILES, GROUPS], F32, name="mass_parts")
+        mass = keep.tile([P, C_TILES], F32, name="mass")
+        neg_mass = keep.tile([P, C_TILES], F32, name="neg_mass")
+        warm_in = keep.tile([P, 1], F32, name="warm_in")
+        warm_out = keep.tile([P, 1], F32, name="warm_out")
+        centres = keep.tile([P, C_TILES, D], BF16, name="centres")
+
+        x_raw, v_raw = {}, {}
+
+        def load_x(g, h):
+            x_raw[g, h] = keep.tile([P, PACK, K_PASS], BF16, name="x_raw_%d_%d" % (g, h))
+            rows = x[g * K_PASS : (g + 1) * K_PASS, h * K_PASS : (h + 1) * K_PASS]
+            nc.sync.dma_start(out=x_raw[g, h][:], in_=rows.rearrange("(p t) e -> p t e", t=PACK))
+
+        def load_v(g, n):
+            v_raw[g, n] = keep.tile([P, PACK, N], BF16, name="v_raw_%d_%d" % (g, n))
+            rows = v[g * K_PASS : (g + 1) * K_PASS, n * N : (n + 1) * N]
+            nc.sync.dma_start(out=v_raw[g, n][:], in_=rows.rearrange("(p t) d -> p t d", t=PACK))
+
+        nc.vector.memset(w_plane[:].rearrange("p g n -> p (g n)").bitcast(I32), 0)
+        nc.vector.memset(warm_in[:], 0.0)
+        load_x(0, 0)
+        load_x(0, 1)
+        nc.sync.dma_start(out=w_codes[:].bitcast(I32), in_=w_words.rearrange("g p b -> p g b").bitcast(I32))
+        scale_rows = w_scales.rearrange("g (q r) n -> r q g n", r=4)
+        for r in range(4):
+            nc.scalar.dma_start(out=w_plane[r:P:32, :, :].bitcast(I32), in_=scale_rows[r].bitcast(I32))
+        nc.scalar.dma_start(out=lengths[:], in_=m.rearrange("(g p t) -> p g t", p=P, t=PACK))
+        nc.scalar.activation(out=warm_out[:], in_=warm_in[:], func=ACT.Sigmoid)
+        for g in range(1, GROUPS):
+            load_x(g, 0)
+            load_x(g, 1)
+            load_v(g - 1, 0)
+        load_v(GROUPS - 1, 0)
+        for g in range(GROUPS):
+            load_v(g, 1)
+        load_v(0, 2)
+        load_v(1, 2)
+        nc.sync.dma_start(out=centres[:], in_=c.rearrange("(j p) d -> p j d", p=P))
+        load_v(2, 2)
+        load_v(3, 2)
+
+        x_grouped, x_codes, x_plane, x_bank = {}, {}, {}, {}
+        z_bank, a_t, a_bank = {}, {}, {}
+        r_grouped, r_codes, r_plane = {}, {}, {}
+        v_grouped, v_codes, v_plane = {}, {}, {}
+        s_bank = {}
+
+        def transpose_x(i):
+            g, h, tp = i // 4, (i // 2) % 2, i % 2
+            x_bank[i] = bank(X_BANKS[i % len(X_BANKS)])
+            for t in range(2):
+                words = x_raw[g, h][:, 2 * tp + t, :].bitcast(F32)
+                for u in range(2):
+                    col = (2 * t + u) * P
+                    nc.tensor.transpose(x_bank[i][:, col : col + P], words[:, u : 2 * P : 2], ident[:])
+
+        def copy_x(i):
+            g, h, tp = i // 4, (i // 2) % 2, i % 2
+            if tp == 0:
+                x_grouped[g, h] = stage.tile([P, N * PACK], BF16, name="x_grouped", align_bytes=64)
+            half = x_grouped[g, h][:, tp * 1024 : (tp + 1) * 1024].bitcast(F32)
+            nc.scalar.copy(
+                out=half.rearrange("p (t r u) -> p t r u", t=2, u=2),
+                in_=x_bank[i][:].rearrange("p (t u r) -> p t r u", t=2, u=2),
+            )
+
+        def quantize(label, key, grouped, codes, plane, fmt):
+            codes[key] = keep.tile([P, N], U32, name="%s_codes_%d_%d" % (label, key[0], key[1]), align_bytes=64)
+            plane[key] = keep.tile([P, N], U8, name="%s_plane_%d_%d" % (label, key[0], key[1]), align_bytes=64)
+            nc.vector.quantize_mx(out=codes[key][:].bitcast(fmt), scales=plane[key][:], in_=grouped[key][:])
+
+        def logits(q):
+            g, j = q // C_TILES, q % C_TILES
+            z_bank[q] = bank(Z_BANKS[q % 2])
+            for h in range(E_PASSES):
+                nc.tensor.matmul_mx(
+                    out=z_bank[q][:],
+                    lhsT=w_codes[:, h, 2 * P * j : 2 * P * (j + 1)].bitcast(E2M1),
+                    lhsT_scale=w_plane[:, h, P * j : P * (j + 1)],
+                    rhs=x_codes[g, h][:].bitcast(E4M3),
+                    rhs_scale=x_plane[g, h][:],
+                    start=(h == 0),
+                    stop=(h == E_PASSES - 1),
+                )
+
+        def sigmoid(q):
+            g, j = q // C_TILES, q % C_TILES
+            a_t[q] = stage.tile([P, N], F32, name="a_t")
+            nc.scalar.activation(out=a_t[q][:], in_=z_bank[q][:], func=ACT.Sigmoid, accum_out=mass_parts[:, j, g : g + 1])
+
+        def transpose_a(q):
+            a_bank[q] = bank(A_BANKS[q % 2])
+            for t in range(PACK):
+                nc.tensor.transpose(a_bank[q][:, t * P : (t + 1) * P], a_t[q][:, t * P : (t + 1) * P], ident[:])
+
+        def weigh(q):
+            g, j = q // C_TILES, q % C_TILES
+            if j == 0:
+                r_grouped[g, 0] = stage.tile([P, C * PACK], BF16, name="r_grouped", align_bytes=64)
+            nc.vector.tensor_tensor(
+                out=r_grouped[g, 0][:, j * N : (j + 1) * N].rearrange("p (c t) -> p c t", t=PACK),
+                in0=a_bank[q][:].rearrange("p (t c) -> p c t", t=PACK),
+                in1=lengths[:, g, :].unsqueeze(1).to_broadcast([P, P, PACK]),
+                op=ALU.mult,
+            )
+
+        def interleave_v(piece, on_vector):
+            unit, part = piece // V_PIECES, piece % V_PIECES
+            g, n = unit % GROUPS, unit // GROUPS
+            if part == 0:
+                v_grouped[g, n] = stage.tile([P, N * PACK], BF16, name="v_grouped", align_bytes=64)
+            dst = v_grouped[g, n][:, part * V_COLS * PACK : (part + 1) * V_COLS * PACK]
+            dst = dst.rearrange("p (c i t) -> p c t i", i=4, t=PACK)
+            src = v_raw[g, n][:, :, part * V_COLS : (part + 1) * V_COLS].rearrange("p t (c i) -> p c t i", i=4)
+            if on_vector:
+                nc.vector.tensor_copy(out=dst, in_=src)
+            else:
+                nc.scalar.copy(out=dst, in_=src)
+
+        def quantize_v(unit):
+            quantize("v", (unit % GROUPS, unit // GROUPS), v_grouped, v_codes, v_plane, E4M3)
+
+        def pool_pass(n, j, g):
+            if g == 0:
+                s_bank[n, j] = bank(S_BANKS[n][j])
+            nc.tensor.matmul_mx(
+                out=s_bank[n, j][:],
+                lhsT=r_codes[g, 0][:, P * j : P * (j + 1)].bitcast(E5M2),
+                lhsT_scale=r_plane[g, 0][:, P * j : P * (j + 1)],
+                rhs=v_codes[g, n][:].bitcast(E4M3),
+                rhs_scale=v_plane[g, n][:],
+                start=(g == 0),
+                stop=(g == GROUPS - 1),
+            )
+
+        def finish(n, j):
+            result = stage.tile([P, N], F32, name="result", bufs=4)
+            nc.vector.scalar_tensor_tensor(
+                out=result[:],
+                in0=centres[:, j, n * N : (n + 1) * N],
+                scalar=neg_mass[:, j : j + 1],
+                in1=s_bank[n, j][:],
+                op0=ALU.mult,
+                op1=ALU.add,
+            )
+            nc.sync.dma_start(out=out[j * P : (j + 1) * P, n * N : (n + 1) * N], in_=result[:])
+
+        for i in range(X_AHEAD):
+            transpose_x(i)
+            copy_x(i)
+            if i % 2 == 1 and i < X_AHEAD - 1:
+                quantize("x", (i // 4, (i // 2) % 2), x_grouped, x_codes, x_plane, E4M3)
+
+        for q in range(STEPS):
+            i = q + X_AHEAD
+            logits(q)
+            if i < STEPS:
+                transpose_x(i)
+            if q >= 2:
+                weigh(q - 2)
+            if q >= 1:
+                transpose_a(q - 1)
+            sigmoid(q)
+            if i < STEPS:
+                copy_x(i)
+            if i - 1 < STEPS and (i - 1) % 2 == 1:
+                quantize("x", ((i - 1) // 4, ((i - 1) // 2) % 2), x_grouped, x_codes, x_plane, E4M3)
+            if q >= 2 and q % 2 == 0:
+                quantize_v(q // 2 - 1)
+            interleave_v(2 * q, True)
+            interleave_v(2 * q + 1, False)
+            if q >= 2 and (q - 2) % C_TILES == C_TILES - 1:
+                quantize("r", ((q - 2) // C_TILES, 0), r_grouped, r_codes, r_plane, E5M2)
+
+        last = STEPS - 1
+        for j in range(C_TILES):
+            pool_pass(0, j, 0)
+        weigh(last - 1)
+        transpose_a(last)
+        quantize_v(7)
+        weigh(last)
+        nc.vector.tensor_reduce(out=mass[:], in_=mass_parts[:], axis=mybir.AxisListType.X, op=ALU.add)
+        for piece in range(32, 36):
+            interleave_v(piece, False)
+        interleave_v(36, True)
+        quantize("r", (GROUPS - 1, 0), r_grouped, r_codes, r_plane, E5M2)
+        nc.vector.tensor_scalar(out=neg_mass[:], in0=mass[:], scalar1=-1.0, scalar2=None, op0=ALU.mult)
+        for piece in range(37, 40):
+            interleave_v(piece, True)
+        quantize_v(8)
+        for g in range(1, GROUPS):
+            for j in range(C_TILES):
+                pool_pass(0, j, g)
+        for piece in range(40, 44):
+            interleave_v(piece, False)
+        finish(0, 0)
+        quantize_v(9)
+        finish(0, 1)
+        for piece in range(44, 48):
+            interleave_v(piece, False)
+        finish(0, 2)
+        quantize_v(10)
+        finish(0, 3)
+        for n in range(1, D_TILES):
+            for j in range(C_TILES):
+                for g in range(GROUPS):
+                    pool_pass(n, j, g)
+                finish(n, j)
+                if n == 1 and j == 1:
+                    quantize_v(11)

@@ -14,7 +14,7 @@ U8 = mybir.dt.uint8
 E4M3 = mybir.dt.float8_e4m3fn_x4
 E5M2 = mybir.dt.float8_e5m2_x4
 E2M1 = mybir.dt.float4_e2m1fn_x4
-ACT = mybir.ActivationFunctionType
+SIGMOID = mybir.ActivationFunctionType.Sigmoid
 ALU = mybir.AluOpType
 
 P = 128
@@ -25,21 +25,29 @@ GROUPS = T // K_PASS
 E_PASSES = E // K_PASS
 C_TILES = C // P
 D_TILES = D // N
-STEPS = GROUPS * C_TILES
+TILES = GROUPS * C_TILES
+STEPS = TILES // 2
+V_UNITS = GROUPS * D_TILES
+
 X_AHEAD = 6
-V_PIECES = 4
-V_COLS = N // V_PIECES
+GPSIMD_COLS = 128
+VECTOR_COLS_BESIDE_X = 256
+VECTOR_COLS_AFTER_X = 64
+WOVEN_PASSES = 2
+WARM_UP_MATMULS = 4
+
 X_BANKS = (0, 1, 6)
 Z_BANKS = (2, 3)
 A_BANKS = (4, 5)
-S_BANKS = ((0, 1, 6, 7), (2, 3, 4, 5), (0, 1, 6, 7))
+SPARE_BANK = 7
+S_BANKS = ((7, 1, 6, 0), (4, 5, 2, 3), (7, 1, 6, 0))
 
 
 def tile_netvlad_length_pooling_s9_kernel(tc, x, w_words, w_scales, m, v, c, out):
     nc = tc.nc
     with ExitStack() as ctx:
         keep = ctx.enter_context(tc.tile_pool(name="keep", bufs=1))
-        stage = ctx.enter_context(tc.tile_pool(name="stage", bufs=3))
+        stage = ctx.enter_context(tc.tile_pool(name="stage", bufs=1))
         psum = ctx.enter_context(tc.psum_pool(name="psum", bufs=1))
         ctx.enter_context(tc.manual_schedule())
 
@@ -47,82 +55,57 @@ def tile_netvlad_length_pooling_s9_kernel(tc, x, w_words, w_scales, m, v, c, out
             return psum.tile([P, N], F32, name="bank%d" % b)
 
         ident = keep.tile([P, P], F32, name="ident")
-        make_identity(nc, ident[:])
-
+        zeros = keep.tile([P, N], BF16, name="zeros")
+        table_in = keep.tile([P, 1], F32, name="table_in")
+        table_out = keep.tile([P, 1], F32, name="table_out")
         w_codes = keep.tile([P, E_PASSES, 2 * C], U8, name="w_codes", align_bytes=64)
         w_plane = keep.tile([P, E_PASSES, C], U8, name="w_plane", align_bytes=64)
         lengths = keep.tile([P, GROUPS, PACK], BF16, name="lengths")
+        centres = keep.tile([P, C_TILES, D], BF16, name="centres")
         mass_parts = keep.tile([P, C_TILES, GROUPS], F32, name="mass_parts")
         mass = keep.tile([P, C_TILES], F32, name="mass")
         neg_mass = keep.tile([P, C_TILES], F32, name="neg_mass")
-        warm_in = keep.tile([P, 1], F32, name="warm_in")
-        warm_out = keep.tile([P, 1], F32, name="warm_out")
-        centres = keep.tile([P, C_TILES, D], BF16, name="centres")
 
-        x_raw, v_raw = {}, {}
+        x_raw, x_bank, x_grouped, x_codes, x_plane = {}, {}, {}, {}, {}
+        z_bank, a_t, a_bank, r_grouped, r_codes, r_plane = {}, {}, {}, {}, {}, {}
+        v_raw, v_grouped, v_codes, v_plane, s_bank = {}, {}, {}, {}, {}
 
-        def load_x(g, h):
-            x_raw[g, h] = keep.tile([P, PACK, K_PASS], BF16, name="x_raw_%d_%d" % (g, h))
-            rows = x[g * K_PASS : (g + 1) * K_PASS, h * K_PASS : (h + 1) * K_PASS]
-            nc.sync.dma_start(out=x_raw[g, h][:], in_=rows.rearrange("(p t) e -> p t e", t=PACK))
+        def load_x(g, half):
+            x_raw[g, half] = keep.tile([P, 2, E], BF16, name="x_raw_%d_%d" % (g, half))
+            rows = x[g * K_PASS : (g + 1) * K_PASS, :].rearrange("(p t) e -> p t e", t=PACK)
+            nc.sync.dma_start(out=x_raw[g, half][:], in_=rows[:, 2 * half : 2 * half + 2, :])
 
-        def load_v(g, n):
-            v_raw[g, n] = keep.tile([P, PACK, N], BF16, name="v_raw_%d_%d" % (g, n))
+        def load_v(unit):
+            g, n = unit % GROUPS, unit // GROUPS
+            v_raw[unit] = keep.tile([P, PACK, N], BF16, name="v_raw_%d" % unit)
             rows = v[g * K_PASS : (g + 1) * K_PASS, n * N : (n + 1) * N]
-            nc.sync.dma_start(out=v_raw[g, n][:], in_=rows.rearrange("(p t) d -> p t d", t=PACK))
-
-        nc.vector.memset(w_plane[:].rearrange("p g n -> p (g n)").bitcast(I32), 0)
-        nc.vector.memset(warm_in[:], 0.0)
-        load_x(0, 0)
-        load_x(0, 1)
-        nc.sync.dma_start(out=w_codes[:].bitcast(I32), in_=w_words.rearrange("g p b -> p g b").bitcast(I32))
-        scale_rows = w_scales.rearrange("g (q r) n -> r q g n", r=4)
-        for r in range(4):
-            nc.scalar.dma_start(out=w_plane[r:P:32, :, :].bitcast(I32), in_=scale_rows[r].bitcast(I32))
-        nc.scalar.dma_start(out=lengths[:], in_=m.rearrange("(g p t) -> p g t", p=P, t=PACK))
-        nc.scalar.activation(out=warm_out[:], in_=warm_in[:], func=ACT.Sigmoid)
-        for g in range(1, GROUPS):
-            load_x(g, 0)
-            load_x(g, 1)
-            load_v(g - 1, 0)
-        load_v(GROUPS - 1, 0)
-        for g in range(GROUPS):
-            load_v(g, 1)
-        load_v(0, 2)
-        load_v(1, 2)
-        nc.sync.dma_start(out=centres[:], in_=c.rearrange("(j p) d -> p j d", p=P))
-        load_v(2, 2)
-        load_v(3, 2)
-
-        x_grouped, x_codes, x_plane, x_bank = {}, {}, {}, {}
-        z_bank, a_t, a_bank = {}, {}, {}
-        r_grouped, r_codes, r_plane = {}, {}, {}
-        v_grouped, v_codes, v_plane = {}, {}, {}
-        s_bank = {}
+            nc.sync.dma_start(out=v_raw[unit][:], in_=rows.rearrange("(p t) d -> p t d", t=PACK))
 
         def transpose_x(i):
-            g, h, tp = i // 4, (i // 2) % 2, i % 2
+            g, half, h = i // 4, (i // 2) % 2, i % 2
             x_bank[i] = bank(X_BANKS[i % len(X_BANKS)])
             for t in range(2):
-                words = x_raw[g, h][:, 2 * tp + t, :].bitcast(F32)
+                words = x_raw[g, half][:, t, h * K_PASS : (h + 1) * K_PASS].bitcast(F32)
                 for u in range(2):
                     col = (2 * t + u) * P
                     nc.tensor.transpose(x_bank[i][:, col : col + P], words[:, u : 2 * P : 2], ident[:])
 
         def copy_x(i):
-            g, h, tp = i // 4, (i // 2) % 2, i % 2
-            if tp == 0:
-                x_grouped[g, h] = stage.tile([P, N * PACK], BF16, name="x_grouped", align_bytes=64)
-            half = x_grouped[g, h][:, tp * 1024 : (tp + 1) * 1024].bitcast(F32)
+            x_grouped[i] = stage.tile([P, 2 * P * PACK], BF16, name="x_grouped", bufs=4, align_bytes=64)
             nc.scalar.copy(
-                out=half.rearrange("p (t r u) -> p t r u", t=2, u=2),
+                out=x_grouped[i][:].bitcast(F32).rearrange("p (t r u) -> p t r u", t=2, u=2),
                 in_=x_bank[i][:].rearrange("p (t u r) -> p t r u", t=2, u=2),
             )
 
-        def quantize(label, key, grouped, codes, plane, fmt):
-            codes[key] = keep.tile([P, N], U32, name="%s_codes_%d_%d" % (label, key[0], key[1]), align_bytes=64)
-            plane[key] = keep.tile([P, N], U8, name="%s_plane_%d_%d" % (label, key[0], key[1]), align_bytes=64)
-            nc.vector.quantize_mx(out=codes[key][:].bitcast(fmt), scales=plane[key][:], in_=grouped[key][:])
+        def quantize_x(i):
+            g, half, h = i // 4, (i // 2) % 2, i % 2
+            if half == 0:
+                x_codes[g, h] = keep.tile([P, N], U32, name="x_codes_%d_%d" % (g, h), align_bytes=64)
+                x_plane[g, h] = keep.tile([P, N], U8, name="x_plane_%d_%d" % (g, h), align_bytes=64)
+            cols = slice(half * 2 * P, (half + 1) * 2 * P)
+            nc.vector.quantize_mx(
+                out=x_codes[g, h][:, cols].bitcast(E4M3), scales=x_plane[g, h][:, cols], in_=x_grouped[i][:]
+            )
 
         def logits(q):
             g, j = q // C_TILES, q % C_TILES
@@ -140,56 +123,75 @@ def tile_netvlad_length_pooling_s9_kernel(tc, x, w_words, w_scales, m, v, c, out
 
         def sigmoid(q):
             g, j = q // C_TILES, q % C_TILES
-            a_t[q] = stage.tile([P, N], F32, name="a_t")
-            nc.scalar.activation(out=a_t[q][:], in_=z_bank[q][:], func=ACT.Sigmoid, accum_out=mass_parts[:, j, g : g + 1])
+            a_t[q] = stage.tile([P, N], F32, name="a_t", bufs=4)
+            nc.scalar.activation(
+                out=a_t[q][:], in_=z_bank[q][:], func=SIGMOID, accum_out=mass_parts[:, j, g : g + 1]
+            )
 
         def transpose_a(q):
-            a_bank[q] = bank(A_BANKS[q % 2])
+            a_bank[q] = bank((A_BANKS if q < TILES - 2 else Z_BANKS)[q % 2])
             for t in range(PACK):
-                nc.tensor.transpose(a_bank[q][:, t * P : (t + 1) * P], a_t[q][:, t * P : (t + 1) * P], ident[:])
+                cols = slice(t * P, (t + 1) * P)
+                nc.tensor.transpose(a_bank[q][:, cols], a_t[q][:, cols], ident[:])
 
         def weigh(q):
             g, j = q // C_TILES, q % C_TILES
             if j == 0:
-                r_grouped[g, 0] = stage.tile([P, C * PACK], BF16, name="r_grouped", align_bytes=64)
+                r_grouped[g] = stage.tile([P, C * PACK], BF16, name="r_grouped", bufs=3, align_bytes=64)
             nc.vector.tensor_tensor(
-                out=r_grouped[g, 0][:, j * N : (j + 1) * N].rearrange("p (c t) -> p c t", t=PACK),
+                out=r_grouped[g][:, j * P * PACK : (j + 1) * P * PACK].rearrange("p (c t) -> p c t", t=PACK),
                 in0=a_bank[q][:].rearrange("p (t c) -> p c t", t=PACK),
                 in1=lengths[:, g, :].unsqueeze(1).to_broadcast([P, P, PACK]),
                 op=ALU.mult,
             )
 
-        def interleave_v(piece, on_vector):
-            unit, part = piece // V_PIECES, piece % V_PIECES
-            g, n = unit % GROUPS, unit // GROUPS
-            if part == 0:
-                v_grouped[g, n] = stage.tile([P, N * PACK], BF16, name="v_grouped", align_bytes=64)
-            dst = v_grouped[g, n][:, part * V_COLS * PACK : (part + 1) * V_COLS * PACK]
-            dst = dst.rearrange("p (c i t) -> p c t i", i=4, t=PACK)
-            src = v_raw[g, n][:, :, part * V_COLS : (part + 1) * V_COLS].rearrange("p t (c i) -> p c t i", i=4)
-            if on_vector:
-                nc.vector.tensor_copy(out=dst, in_=src)
-            else:
-                nc.scalar.copy(out=dst, in_=src)
+        def quantize_r(g):
+            r_codes[g] = keep.tile([P, C], U32, name="r_codes_%d" % g, align_bytes=64)
+            r_plane[g] = keep.tile([P, C], U8, name="r_plane_%d" % g, align_bytes=64)
+            nc.vector.quantize_mx(out=r_codes[g][:].bitcast(E5M2), scales=r_plane[g][:], in_=r_grouped[g][:])
+
+        def open_v(unit):
+            v_grouped[unit] = stage.tile([P, N * PACK], BF16, name="v_grouped", bufs=2, align_bytes=64)
+
+        def interleave_v_gpsimd(unit):
+            nc.gpsimd.tensor_scalar(
+                out=v_grouped[unit][:, : GPSIMD_COLS * PACK].rearrange("p (d t) -> p d t", t=PACK),
+                in0=v_raw[unit][:, :, :GPSIMD_COLS].rearrange("p t d -> p d t"),
+                scalar1=1.0,
+                scalar2=0.0,
+                op0=ALU.mult,
+                op1=ALU.add,
+            )
+
+        def interleave_v(copy, unit, lo, hi):
+            copy(
+                out=v_grouped[unit][:, lo * PACK : hi * PACK].rearrange("p (d i t) -> p d t i", i=4, t=PACK),
+                in_=v_raw[unit][:, :, lo:hi].rearrange("p t (d i) -> p d t i", i=4),
+            )
 
         def quantize_v(unit):
-            quantize("v", (unit % GROUPS, unit // GROUPS), v_grouped, v_codes, v_plane, E4M3)
+            v_codes[unit] = keep.tile([P, N], U32, name="v_codes_%d" % unit, align_bytes=64)
+            v_plane[unit] = keep.tile([P, N], U8, name="v_plane_%d" % unit, align_bytes=64)
+            nc.vector.quantize_mx(
+                out=v_codes[unit][:].bitcast(E4M3), scales=v_plane[unit][:], in_=v_grouped[unit][:]
+            )
 
         def pool_pass(n, j, g):
             if g == 0:
                 s_bank[n, j] = bank(S_BANKS[n][j])
+            unit = n * GROUPS + g
             nc.tensor.matmul_mx(
                 out=s_bank[n, j][:],
-                lhsT=r_codes[g, 0][:, P * j : P * (j + 1)].bitcast(E5M2),
-                lhsT_scale=r_plane[g, 0][:, P * j : P * (j + 1)],
-                rhs=v_codes[g, n][:].bitcast(E4M3),
-                rhs_scale=v_plane[g, n][:],
+                lhsT=r_codes[g][:, P * j : P * (j + 1)].bitcast(E5M2),
+                lhsT_scale=r_plane[g][:, P * j : P * (j + 1)],
+                rhs=v_codes[unit][:].bitcast(E4M3),
+                rhs_scale=v_plane[unit][:],
                 start=(g == 0),
                 stop=(g == GROUPS - 1),
             )
 
         def finish(n, j):
-            result = stage.tile([P, N], F32, name="result", bufs=4)
+            result = stage.tile([P, N], F32, name="result", bufs=6)
             nc.vector.scalar_tensor_tensor(
                 out=result[:],
                 in0=centres[:, j, n * N : (n + 1) * N],
@@ -200,66 +202,124 @@ def tile_netvlad_length_pooling_s9_kernel(tc, x, w_words, w_scales, m, v, c, out
             )
             nc.sync.dma_start(out=out[j * P : (j + 1) * P, n * N : (n + 1) * N], in_=result[:])
 
+        nc.vector.memset(w_plane[:].rearrange("p h n -> p (h n)").bitcast(I32), 0)
+        nc.vector.memset(table_in[:], 0.0)
+        nc.vector.memset(zeros[:], 0.0)
+        make_identity(nc, ident[:])
+
+        load_x(0, 0)
+        load_x(0, 1)
+        load_x(1, 0)
+        nc.sync.dma_start(out=w_codes[:].bitcast(I32), in_=w_words.rearrange("h p b -> p h b").bitcast(I32))
+        scale_rows = w_scales.rearrange("h (q r) n -> r q h n", r=4)
+        for r in range(4):
+            nc.scalar.dma_start(out=w_plane[r:P:32, :, :].bitcast(I32), in_=scale_rows[r].bitcast(I32))
+        nc.scalar.activation(out=table_out[:], in_=table_in[:], func=SIGMOID)
+        load_v(0)
+        load_x(1, 1)
+        load_v(1)
+        nc.sync.dma_start(out=lengths[:], in_=m.rearrange("(g p t) -> p g t", p=P, t=PACK))
+        for i in range(4):
+            load_x(2 + i // 2, i % 2)
+            load_v(2 + i)
+        for unit in range(6, V_UNITS - 2):
+            load_v(unit)
+        nc.sync.dma_start(out=centres[:], in_=c.rearrange("(j p) d -> p j d", p=P))
+        for unit in range(V_UNITS - 2, V_UNITS):
+            load_v(unit)
+
+        scratch = bank(SPARE_BANK)
+        for i in range(WARM_UP_MATMULS):
+            nc.tensor.matmul(scratch[:], lhsT=zeros[:, :P], rhs=zeros[:], start=True, stop=True)
+
         for i in range(X_AHEAD):
             transpose_x(i)
+            if i == E_PASSES - 1:
+                nc.tensor.matmul(scratch[:], lhsT=zeros[:, :P], rhs=zeros[:], start=True, stop=True)
             copy_x(i)
-            if i % 2 == 1 and i < X_AHEAD - 1:
-                quantize("x", (i // 4, (i // 2) % 2), x_grouped, x_codes, x_plane, E4M3)
+            if i < X_AHEAD - 2:
+                quantize_x(i)
 
-        for q in range(STEPS):
-            i = q + X_AHEAD
-            logits(q)
-            if i < STEPS:
-                transpose_x(i)
-            if q >= 2:
-                weigh(q - 2)
-            if q >= 1:
-                transpose_a(q - 1)
-            sigmoid(q)
-            if i < STEPS:
-                copy_x(i)
-            if i - 1 < STEPS and (i - 1) % 2 == 1:
-                quantize("x", ((i - 1) // 4, ((i - 1) // 2) % 2), x_grouped, x_codes, x_plane, E4M3)
-            if q >= 2 and q % 2 == 0:
-                quantize_v(q // 2 - 1)
-            interleave_v(2 * q, True)
-            interleave_v(2 * q + 1, False)
-            if q >= 2 and (q - 2) % C_TILES == C_TILES - 1:
-                quantize("r", ((q - 2) // C_TILES, 0), r_grouped, r_codes, r_plane, E5M2)
-
-        last = STEPS - 1
-        for j in range(C_TILES):
-            pool_pass(0, j, 0)
-        weigh(last - 1)
-        transpose_a(last)
-        quantize_v(7)
-        weigh(last)
-        nc.vector.tensor_reduce(out=mass[:], in_=mass_parts[:], axis=mybir.AxisListType.X, op=ALU.add)
-        for piece in range(32, 36):
-            interleave_v(piece, False)
-        interleave_v(36, True)
-        quantize("r", (GROUPS - 1, 0), r_grouped, r_codes, r_plane, E5M2)
-        nc.vector.tensor_scalar(out=neg_mass[:], in0=mass[:], scalar1=-1.0, scalar2=None, op0=ALU.mult)
-        for piece in range(37, 40):
-            interleave_v(piece, True)
-        quantize_v(8)
-        for g in range(1, GROUPS):
-            for j in range(C_TILES):
-                pool_pass(0, j, g)
-        for piece in range(40, 44):
-            interleave_v(piece, False)
-        finish(0, 0)
-        quantize_v(9)
-        finish(0, 1)
-        for piece in range(44, 48):
-            interleave_v(piece, False)
-        finish(0, 2)
-        quantize_v(10)
-        finish(0, 3)
-        for n in range(1, D_TILES):
-            for j in range(C_TILES):
-                for g in range(GROUPS):
+        first_woven_step = (TILES - X_AHEAD) // 2
+        woven = [(0, j, g) for g in range(GROUPS - 1) for j in range(C_TILES)]
+        for k in range(STEPS + 1):
+            now = (2 * k, 2 * k + 1)
+            x_now = [q + X_AHEAD for q in now if q + X_AHEAD < TILES]
+            open_v(k)
+            if k < 2:
+                vector_from, scalar_from = 0, N
+            else:
+                interleave_v_gpsimd(k)
+                vector_from = GPSIMD_COLS
+                scalar_from = vector_from + (VECTOR_COLS_BESIDE_X if x_now else VECTOR_COLS_AFTER_X)
+            if k < STEPS:
+                for q in now:
+                    logits(q)
+            if k >= first_woven_step:
+                first = WOVEN_PASSES * (k - first_woven_step)
+                for n, j, g in woven[first : first + WOVEN_PASSES] if k < STEPS else woven[first:]:
                     pool_pass(n, j, g)
-                finish(n, j)
-                if n == 1 and j == 1:
-                    quantize_v(11)
+            for i in x_now:
+                transpose_x(i)
+            if k >= 2:
+                for q in now:
+                    weigh(q - 4)
+            if k >= 1:
+                for q in now:
+                    transpose_a(q - 2)
+            if k < STEPS:
+                for q in now:
+                    sigmoid(q)
+            for q in now:
+                if q + X_AHEAD - 2 < TILES:
+                    quantize_x(q + X_AHEAD - 2)
+            interleave_v(nc.vector.tensor_copy, k, vector_from, scalar_from)
+            for i in x_now:
+                copy_x(i)
+            if scalar_from < N:
+                interleave_v(nc.scalar.copy, k, scalar_from, N)
+            if k >= 3 and k % 2 == 1:
+                quantize_r((k - 3) // 2)
+            if k >= 1:
+                quantize_v(k - 1)
+
+        unit = STEPS + 1
+        open_v(unit)
+        interleave_v_gpsimd(unit)
+        weigh(TILES - 2)
+        weigh(TILES - 1)
+        interleave_v(nc.scalar.copy, unit, GPSIMD_COLS + VECTOR_COLS_AFTER_X, N)
+        nc.vector.tensor_reduce(out=mass[:], in_=mass_parts[:], axis=mybir.AxisListType.X, op=ALU.add)
+        quantize_r(GROUPS - 1)
+        nc.vector.tensor_scalar(out=neg_mass[:], in0=mass[:], scalar1=-1.0, scalar2=None, op0=ALU.mult)
+        interleave_v(nc.vector.tensor_copy, unit, GPSIMD_COLS, GPSIMD_COLS + VECTOR_COLS_AFTER_X)
+        quantize_v(unit - 1)
+
+        for g in range(GROUPS - 1):
+            for j in range(2):
+                pool_pass(1, j, g)
+        for j in range(C_TILES):
+            pool_pass(0, j, GROUPS - 1)
+
+        for half in range(2):
+            unit = V_UNITS - 2 + half
+            open_v(unit)
+            interleave_v_gpsimd(unit)
+            interleave_v(nc.scalar.copy, unit, GPSIMD_COLS, N)
+            finish(0, 2 * half)
+            finish(0, 2 * half + 1)
+            quantize_v(unit - 1)
+        for j in range(C_TILES):
+            for g in range(GROUPS - 1 if j < 2 else 0, GROUPS):
+                pool_pass(1, j, g)
+            finish(1, j)
+            if j == 1:
+                quantize_v(V_UNITS - 1)
+
+        for g in range(2):
+            for j in range(C_TILES):
+                pool_pass(2, j, g)
+        for j in range(C_TILES):
+            for g in range(2, GROUPS):
+                pool_pass(2, j, g)
+            finish(2, j)

from contextlib import ExitStack

import concourse.mybir as mybir
from concourse.masks import make_identity

T, E, C, D = 2048, 1024, 512, 1536
FLOPS = 2 * T * E * C + 2 * T * C * D

F32 = mybir.dt.float32
BF16 = mybir.dt.bfloat16
I32 = mybir.dt.int32
U32 = mybir.dt.uint32
U8 = mybir.dt.uint8
E4M3 = mybir.dt.float8_e4m3fn_x4
E5M2 = mybir.dt.float8_e5m2_x4
E2M1 = mybir.dt.float4_e2m1fn_x4
SIGMOID = mybir.ActivationFunctionType.Sigmoid
ALU = mybir.AluOpType

P = 128
PACK = 4
K_PASS = P * PACK
N = 512
GROUPS = T // K_PASS
E_PASSES = E // K_PASS
C_TILES = C // P
D_TILES = D // N
TILES = GROUPS * C_TILES
STEPS = TILES // 2
V_UNITS = GROUPS * D_TILES

X_AHEAD = 6
GPSIMD_COLS = 128
VECTOR_COLS_BESIDE_X = 256
VECTOR_COLS_AFTER_X = 64
WOVEN_PASSES = 2
WARM_UP_MATMULS = 4

X_BANKS = (0, 1, 6)
Z_BANKS = (2, 3)
A_BANKS = (4, 5)
SPARE_BANK = 7
S_BANKS = ((7, 1, 6, 0), (4, 5, 2, 3), (7, 1, 6, 0))


def tile_netvlad_length_pooling_s9_kernel(tc, x, w_words, w_scales, m, v, c, out):
    nc = tc.nc
    with ExitStack() as ctx:
        keep = ctx.enter_context(tc.tile_pool(name="keep", bufs=1))
        stage = ctx.enter_context(tc.tile_pool(name="stage", bufs=1))
        psum = ctx.enter_context(tc.psum_pool(name="psum", bufs=1))
        ctx.enter_context(tc.manual_schedule())

        def bank(b):
            return psum.tile([P, N], F32, name="bank%d" % b)

        ident = keep.tile([P, P], F32, name="ident")
        zeros = keep.tile([P, N], BF16, name="zeros")
        table_in = keep.tile([P, 1], F32, name="table_in")
        table_out = keep.tile([P, 1], F32, name="table_out")
        w_codes = keep.tile([P, E_PASSES, 2 * C], U8, name="w_codes", align_bytes=64)
        w_plane = keep.tile([P, E_PASSES, C], U8, name="w_plane", align_bytes=64)
        lengths = keep.tile([P, GROUPS, PACK], BF16, name="lengths")
        centres = keep.tile([P, C_TILES, D], BF16, name="centres")
        mass_parts = keep.tile([P, C_TILES, GROUPS], F32, name="mass_parts")
        mass = keep.tile([P, C_TILES], F32, name="mass")
        neg_mass = keep.tile([P, C_TILES], F32, name="neg_mass")

        x_raw, x_bank, x_grouped, x_codes, x_plane = {}, {}, {}, {}, {}
        z_bank, a_t, a_bank, r_grouped, r_codes, r_plane = {}, {}, {}, {}, {}, {}
        v_raw, v_grouped, v_codes, v_plane, s_bank = {}, {}, {}, {}, {}

        def load_x(g, half):
            x_raw[g, half] = keep.tile([P, 2, E], BF16, name="x_raw_%d_%d" % (g, half))
            rows = x[g * K_PASS : (g + 1) * K_PASS, :].rearrange("(p t) e -> p t e", t=PACK)
            nc.sync.dma_start(out=x_raw[g, half][:], in_=rows[:, 2 * half : 2 * half + 2, :])

        def load_v(unit):
            g, n = unit % GROUPS, unit // GROUPS
            v_raw[unit] = keep.tile([P, PACK, N], BF16, name="v_raw_%d" % unit)
            rows = v[g * K_PASS : (g + 1) * K_PASS, n * N : (n + 1) * N]
            nc.sync.dma_start(out=v_raw[unit][:], in_=rows.rearrange("(p t) d -> p t d", t=PACK))

        def transpose_x(i):
            g, half, h = i // 4, (i // 2) % 2, i % 2
            x_bank[i] = bank(X_BANKS[i % len(X_BANKS)])
            for t in range(2):
                words = x_raw[g, half][:, t, h * K_PASS : (h + 1) * K_PASS].bitcast(F32)
                for u in range(2):
                    col = (2 * t + u) * P
                    nc.tensor.transpose(x_bank[i][:, col : col + P], words[:, u : 2 * P : 2], ident[:])

        def copy_x(i):
            x_grouped[i] = stage.tile([P, 2 * P * PACK], BF16, name="x_grouped", bufs=4, align_bytes=64)
            nc.scalar.copy(
                out=x_grouped[i][:].bitcast(F32).rearrange("p (t r u) -> p t r u", t=2, u=2),
                in_=x_bank[i][:].rearrange("p (t u r) -> p t r u", t=2, u=2),
            )

        def quantize_x(i):
            g, half, h = i // 4, (i // 2) % 2, i % 2
            if half == 0:
                x_codes[g, h] = keep.tile([P, N], U32, name="x_codes_%d_%d" % (g, h), align_bytes=64)
                x_plane[g, h] = keep.tile([P, N], U8, name="x_plane_%d_%d" % (g, h), align_bytes=64)
            cols = slice(half * 2 * P, (half + 1) * 2 * P)
            nc.vector.quantize_mx(
                out=x_codes[g, h][:, cols].bitcast(E4M3), scales=x_plane[g, h][:, cols], in_=x_grouped[i][:]
            )

        def logits(q):
            g, j = q // C_TILES, q % C_TILES
            z_bank[q] = bank(Z_BANKS[q % 2])
            for h in range(E_PASSES):
                nc.tensor.matmul_mx(
                    out=z_bank[q][:],
                    lhsT=w_codes[:, h, 2 * P * j : 2 * P * (j + 1)].bitcast(E2M1),
                    lhsT_scale=w_plane[:, h, P * j : P * (j + 1)],
                    rhs=x_codes[g, h][:].bitcast(E4M3),
                    rhs_scale=x_plane[g, h][:],
                    start=(h == 0),
                    stop=(h == E_PASSES - 1),
                )

        def sigmoid(q):
            g, j = q // C_TILES, q % C_TILES
            a_t[q] = stage.tile([P, N], F32, name="a_t", bufs=4)
            nc.scalar.activation(
                out=a_t[q][:], in_=z_bank[q][:], func=SIGMOID, accum_out=mass_parts[:, j, g : g + 1]
            )

        def transpose_a(q):
            a_bank[q] = bank((A_BANKS if q < TILES - 2 else Z_BANKS)[q % 2])
            for t in range(PACK):
                cols = slice(t * P, (t + 1) * P)
                nc.tensor.transpose(a_bank[q][:, cols], a_t[q][:, cols], ident[:])

        def weigh(q):
            g, j = q // C_TILES, q % C_TILES
            if j == 0:
                r_grouped[g] = stage.tile([P, C * PACK], BF16, name="r_grouped", bufs=3, align_bytes=64)
            nc.vector.tensor_tensor(
                out=r_grouped[g][:, j * P * PACK : (j + 1) * P * PACK].rearrange("p (c t) -> p c t", t=PACK),
                in0=a_bank[q][:].rearrange("p (t c) -> p c t", t=PACK),
                in1=lengths[:, g, :].unsqueeze(1).to_broadcast([P, P, PACK]),
                op=ALU.mult,
            )

        def quantize_r(g):
            r_codes[g] = keep.tile([P, C], U32, name="r_codes_%d" % g, align_bytes=64)
            r_plane[g] = keep.tile([P, C], U8, name="r_plane_%d" % g, align_bytes=64)
            nc.vector.quantize_mx(out=r_codes[g][:].bitcast(E5M2), scales=r_plane[g][:], in_=r_grouped[g][:])

        def open_v(unit):
            v_grouped[unit] = stage.tile([P, N * PACK], BF16, name="v_grouped", bufs=2, align_bytes=64)

        def interleave_v_gpsimd(unit):
            nc.gpsimd.tensor_scalar(
                out=v_grouped[unit][:, : GPSIMD_COLS * PACK].rearrange("p (d t) -> p d t", t=PACK),
                in0=v_raw[unit][:, :, :GPSIMD_COLS].rearrange("p t d -> p d t"),
                scalar1=1.0,
                scalar2=0.0,
                op0=ALU.mult,
                op1=ALU.add,
            )

        def interleave_v(copy, unit, lo, hi):
            copy(
                out=v_grouped[unit][:, lo * PACK : hi * PACK].rearrange("p (d i t) -> p d t i", i=4, t=PACK),
                in_=v_raw[unit][:, :, lo:hi].rearrange("p t (d i) -> p d t i", i=4),
            )

        def quantize_v(unit):
            v_codes[unit] = keep.tile([P, N], U32, name="v_codes_%d" % unit, align_bytes=64)
            v_plane[unit] = keep.tile([P, N], U8, name="v_plane_%d" % unit, align_bytes=64)
            nc.vector.quantize_mx(
                out=v_codes[unit][:].bitcast(E4M3), scales=v_plane[unit][:], in_=v_grouped[unit][:]
            )

        def pool_pass(n, j, g):
            if g == 0:
                s_bank[n, j] = bank(S_BANKS[n][j])
            unit = n * GROUPS + g
            nc.tensor.matmul_mx(
                out=s_bank[n, j][:],
                lhsT=r_codes[g][:, P * j : P * (j + 1)].bitcast(E5M2),
                lhsT_scale=r_plane[g][:, P * j : P * (j + 1)],
                rhs=v_codes[unit][:].bitcast(E4M3),
                rhs_scale=v_plane[unit][:],
                start=(g == 0),
                stop=(g == GROUPS - 1),
            )

        def finish(n, j):
            result = stage.tile([P, N], F32, name="result", bufs=6)
            nc.vector.scalar_tensor_tensor(
                out=result[:],
                in0=centres[:, j, n * N : (n + 1) * N],
                scalar=neg_mass[:, j : j + 1],
                in1=s_bank[n, j][:],
                op0=ALU.mult,
                op1=ALU.add,
            )
            nc.sync.dma_start(out=out[j * P : (j + 1) * P, n * N : (n + 1) * N], in_=result[:])

        nc.vector.memset(w_plane[:].rearrange("p h n -> p (h n)").bitcast(I32), 0)
        nc.vector.memset(table_in[:], 0.0)
        nc.vector.memset(zeros[:], 0.0)
        make_identity(nc, ident[:])

        load_x(0, 0)
        load_x(0, 1)
        load_x(1, 0)
        nc.sync.dma_start(out=w_codes[:].bitcast(I32), in_=w_words.rearrange("h p b -> p h b").bitcast(I32))
        scale_rows = w_scales.rearrange("h (q r) n -> r q h n", r=4)
        for r in range(4):
            nc.scalar.dma_start(out=w_plane[r:P:32, :, :].bitcast(I32), in_=scale_rows[r].bitcast(I32))
        nc.scalar.activation(out=table_out[:], in_=table_in[:], func=SIGMOID)
        load_v(0)
        load_x(1, 1)
        load_v(1)
        nc.sync.dma_start(out=lengths[:], in_=m.rearrange("(g p t) -> p g t", p=P, t=PACK))
        for i in range(4):
            load_x(2 + i // 2, i % 2)
            load_v(2 + i)
        for unit in range(6, V_UNITS - 2):
            load_v(unit)
        nc.sync.dma_start(out=centres[:], in_=c.rearrange("(j p) d -> p j d", p=P))
        for unit in range(V_UNITS - 2, V_UNITS):
            load_v(unit)

        scratch = bank(SPARE_BANK)
        for i in range(WARM_UP_MATMULS):
            nc.tensor.matmul(scratch[:], lhsT=zeros[:, :P], rhs=zeros[:], start=True, stop=True)

        for i in range(X_AHEAD):
            transpose_x(i)
            if i == E_PASSES - 1:
                nc.tensor.matmul(scratch[:], lhsT=zeros[:, :P], rhs=zeros[:], start=True, stop=True)
            copy_x(i)
            if i < X_AHEAD - 2:
                quantize_x(i)

        first_woven_step = (TILES - X_AHEAD) // 2
        woven = [(0, j, g) for g in range(GROUPS - 1) for j in range(C_TILES)]
        for k in range(STEPS + 1):
            now = (2 * k, 2 * k + 1)
            x_now = [q + X_AHEAD for q in now if q + X_AHEAD < TILES]
            open_v(k)
            if k < 2:
                vector_from, scalar_from = 0, N
            else:
                interleave_v_gpsimd(k)
                vector_from = GPSIMD_COLS
                scalar_from = vector_from + (VECTOR_COLS_BESIDE_X if x_now else VECTOR_COLS_AFTER_X)
            if k < STEPS:
                for q in now:
                    logits(q)
            if k >= first_woven_step:
                first = WOVEN_PASSES * (k - first_woven_step)
                for n, j, g in woven[first : first + WOVEN_PASSES] if k < STEPS else woven[first:]:
                    pool_pass(n, j, g)
            for i in x_now:
                transpose_x(i)
            if k >= 2:
                for q in now:
                    weigh(q - 4)
            if k >= 1:
                for q in now:
                    transpose_a(q - 2)
            if k < STEPS:
                for q in now:
                    sigmoid(q)
            for q in now:
                if q + X_AHEAD - 2 < TILES:
                    quantize_x(q + X_AHEAD - 2)
            interleave_v(nc.vector.tensor_copy, k, vector_from, scalar_from)
            for i in x_now:
                copy_x(i)
            if scalar_from < N:
                interleave_v(nc.scalar.copy, k, scalar_from, N)
            if k >= 3 and k % 2 == 1:
                quantize_r((k - 3) // 2)
            if k >= 1:
                quantize_v(k - 1)

        unit = STEPS + 1
        open_v(unit)
        interleave_v_gpsimd(unit)
        weigh(TILES - 2)
        weigh(TILES - 1)
        interleave_v(nc.scalar.copy, unit, GPSIMD_COLS + VECTOR_COLS_AFTER_X, N)
        nc.vector.tensor_reduce(out=mass[:], in_=mass_parts[:], axis=mybir.AxisListType.X, op=ALU.add)
        quantize_r(GROUPS - 1)
        nc.vector.tensor_scalar(out=neg_mass[:], in0=mass[:], scalar1=-1.0, scalar2=None, op0=ALU.mult)
        interleave_v(nc.vector.tensor_copy, unit, GPSIMD_COLS, GPSIMD_COLS + VECTOR_COLS_AFTER_X)
        quantize_v(unit - 1)

        for g in range(GROUPS - 1):
            for j in range(2):
                pool_pass(1, j, g)
        for j in range(C_TILES):
            pool_pass(0, j, GROUPS - 1)

        for half in range(2):
            unit = V_UNITS - 2 + half
            open_v(unit)
            interleave_v_gpsimd(unit)
            interleave_v(nc.scalar.copy, unit, GPSIMD_COLS, N)
            finish(0, 2 * half)
            finish(0, 2 * half + 1)
            quantize_v(unit - 1)
        for j in range(C_TILES):
            for g in range(GROUPS - 1 if j < 2 else 0, GROUPS):
                pool_pass(1, j, g)
            finish(1, j)
            if j == 1:
                quantize_v(V_UNITS - 1)

        for g in range(2):
            for j in range(C_TILES):
                pool_pass(2, j, g)
        for j in range(C_TILES):
            for g in range(2, GROUPS):
                pool_pass(2, j, g)
            finish(2, j)
